import numpy as np
import ml_dtypes


def mxq(x, axis, fmt="e4m3"):
    dtype, down = {"e4m3": (ml_dtypes.float8_e4m3fn, 7), "e5m2": (ml_dtypes.float8_e5m2, 14)}[fmt]
    v = np.moveaxis(np.asarray(x, np.float32).astype(ml_dtypes.bfloat16).astype(np.float64), axis, -1)
    blocks = v.reshape(v.shape[:-1] + (-1, 32))
    amax = np.abs(blocks).max(-1, keepdims=True)
    byte = np.maximum(np.where(amax > 0, np.frexp(amax)[1] - 1 + 127, 0) - down, 1)
    scale = np.exp2(byte - 127.0)
    codes = (blocks / scale).astype(np.float32).astype(dtype).astype(np.float64)
    return np.moveaxis((codes * scale).reshape(v.shape), -1, axis)


WIDE = False


def mx_kscale(k):
    if not WIDE:
        return np.ones(k)
    levels = np.array([10, -10, 5, -5, 0])
    if k % 512:
        return np.exp2(np.random.permutation(np.resize(levels, k // 32))).repeat(32)
    a = np.empty((k // 512, 16))
    for p in range(k // 512):
        a[p, :8] = np.random.permutation(np.resize(levels, 8))
        for g in range(8):
            far = levels[np.abs(levels - a[p, g]) >= 10]
            a[p, g + 8] = far[np.random.randint(len(far))]
    return np.exp2(a.ravel()).repeat(32)


def f64(x):
    return np.asarray(x).astype(np.float64)


def striped(idx):
    return np.tile(idx.reshape(-1, 16).T, (8, 1)).astype(np.uint16)


def unstriped(offs):
    return offs[:16].T.reshape(-1).astype(np.int64)


def striped8(idx):
    return np.concatenate([x.reshape(-1, 16).T for x in idx]).astype(np.uint16)


def runs(offs, k):
    lists = np.stack([offs[16 * r : 16 * r + 16].T.reshape(-1) for r in range(8)]).astype(np.int64)
    return lists[np.arange(k) % 512 // 64]


def pack_weight(w):
    k, n = w.shape
    w = f64(np.asarray(w, np.float32).astype(ml_dtypes.bfloat16)).reshape(k // 32, 32, n)
    amax = np.abs(w).max(1)
    byte = np.clip(np.where(amax > 0, np.frexp(amax)[1] - 1 + 127 - 7, 1), 1, 254)
    scaled = (w * np.exp2(127.0 - byte)[:, None, :]).reshape(k, n).astype(np.float32)
    words = np.ascontiguousarray(scaled.reshape(k // 512, 128, 4, n).transpose(0, 1, 3, 2)).astype(ml_dtypes.float8_e4m3fn).view(np.uint8)
    return words, np.ascontiguousarray(byte.astype(np.uint8).reshape(k // 512, 16, n))


def unpack_weight(words, scales):
    g, p, n, _ = words.shape
    vals = np.ascontiguousarray(words).view(ml_dtypes.float8_e4m3fn).astype(np.float64) * np.repeat(np.exp2(scales.astype(np.float64) - 127.0), 8, axis=1)[..., None]
    return vals.transpose(0, 1, 3, 2).reshape(g * 512, n)


E2M1 = np.array([0.0, 0.5, 1.0, 1.5, 2.0, 3.0, 4.0, 6.0, -0.0, -0.5, -1.0, -1.5, -2.0, -3.0, -4.0, -6.0])


def pack_fp4(w):
    k, n = w.shape
    w = f64(np.asarray(w, np.float32).astype(ml_dtypes.bfloat16)).reshape(k // 32, 32, n)
    amax = np.abs(w).max(1)
    mant, ex = np.frexp(amax / 6.0)
    byte = np.clip(np.where(amax > 0, np.where(mant > 0.5, ex, ex - 1) + 127, 1), 1, 254)
    scaled = (w * np.exp2(127.0 - byte)[:, None, :]).reshape(k, n).astype(np.float32)
    c = np.ascontiguousarray(scaled.reshape(k // 512, 128, 4, n).transpose(0, 1, 3, 2)).astype(ml_dtypes.float4_e2m1fn).view(np.uint8) & 0xF
    words = (c[..., 0::2] | (c[..., 1::2] << 4)).reshape(k // 512, 128, 2 * n)
    return np.ascontiguousarray(words), np.ascontiguousarray(byte.astype(np.uint8).reshape(k // 512, 16, n))


def unpack_fp4(words, scales):
    g, _, n = scales.shape
    words = np.ascontiguousarray(words).reshape(g, 128, n, 2)
    nib = np.empty((g, 128, n, 4), np.uint8)
    nib[..., 0::2] = words & 0xF
    nib[..., 1::2] = words >> 4
    vals = E2M1[nib] * np.repeat(np.exp2(scales.astype(np.float64) - 127.0), 8, axis=1)[..., None]
    return vals.transpose(0, 1, 3, 2).reshape(g * 512, n)


def sigmoid(v):
    return 1.0 / (1.0 + np.exp(-np.maximum(v, -700.0)))

def planes(y):
    n, m = y.shape
    v = y.astype(np.float32).astype(ml_dtypes.bfloat16).astype(np.float64).reshape(n // 32, 32, m)
    top = np.abs(v).max(1)
    byte = np.clip(np.where(top > 0, np.frexp(top)[1] - 1 + 127 - 7, 1), 1, 254)
    codes = (v * np.exp2(127.0 - byte)[:, None, :]).reshape(n, m).astype(np.float32).astype(ml_dtypes.float8_e4m3fn).view(np.uint8)
    words = codes.reshape(n // 512, 128, 4, m).transpose(0, 1, 3, 2)
    return np.ascontiguousarray(words), np.ascontiguousarray(byte.astype(np.uint8).reshape(n // 512, 16, m))


K, T, S, N, U, H = 512, 2048, 512, 512, 1024, 512


def setup_inputs():
    n = np.random.standard_normal
    s = mx_kscale(K)[:, None]
    u = mx_kscale(H)
    packed_xT = pack_weight(n((K, T)) * s)
    packed_w2 = pack_fp4(n((H, N)) / np.sqrt(H) / u[:, None])
    return {
        "x_words": packed_xT[0],
        "x_scales": packed_xT[1],
        "w1": (n((K, H)) / np.sqrt(K) / s * u).astype(np.float32),
        "w2_words": packed_w2[0],
        "w2_scales": packed_w2[1],
        "pg": n((N, U)).astype(np.float32),
        "offs": striped(np.random.permutation(T)[:S]),
        "nb": striped8(np.stack([np.random.permutation(S) for _ in range(8)])),
        "slot": striped8(np.stack([np.random.permutation(U)[:S] for _ in range(8)])),
    }


def reference(x_words, x_scales, w1, w2_words, w2_scales, pg, offs, nb, slot):
    xq = unpack_weight(x_words, x_scales)[:, unstriped(offs)]
    y = mxq(f64(w1), 0, "e4m3").T @ xq
    z = y - (y[np.arange(H)[:, None], runs(nb, H)])
    h = unpack_fp4(w2_words, w2_scales).T @ mxq(z, 0, "e4m3")
    nw = h + sigmoid(h) * (f64(pg)[np.arange(N)[:, None], runs(slot, N)])
    out = f64(pg).copy()
    out[np.arange(N)[:, None], runs(slot, N)] = nw
    return (out,) + planes(out)

@@ -1,0 +1,192 @@
+from contextlib import ExitStack
+
+import concourse.mybir as mybir
+
+K, T, S, N, U, H = 512, 2048, 512, 512, 1024, 512
+FLOPS = 2 * K * H * S + 2 * H * N * S
+
+F32 = mybir.dt.float32
+BF16 = mybir.dt.bfloat16
+I32 = mybir.dt.int32
+U32 = mybir.dt.uint32
+U16 = mybir.dt.uint16
+U8 = mybir.dt.uint8
+FP8X4 = mybir.dt.float8_e4m3fn_x4
+FP4X4 = mybir.dt.float4_e2m1fn_x4
+ALU = mybir.AluOpType
+ACT = mybir.ActivationFunctionType
+
+P = 128
+PACK = 4
+HALF = S // 2
+QUARTER = S // 4
+CHUNK = U // 4
+
+
+def tile_picked_pagefly_none_po_kernel(
+    tc, x_words, x_scales, w1, w2_words, w2_scales, pg, offs, nb, slot, out_0, out_1, out_2
+):
+    nc = tc.nc
+    with ExitStack() as ctx:
+        keep = ctx.enter_context(tc.tile_pool(name="keep", bufs=1))
+        psum = ctx.enter_context(tc.psum_pool(name="psum", bufs=1))
+
+        offs_t = keep.tile([P, S // 16], U16, name="offs_t")
+        nb_t = keep.tile([P, S // 16], U16, name="nb_t")
+        slot_t = keep.tile([P, S // 16], U16, name="slot_t")
+        xw = keep.tile([P, T], I32, name="xw", align_bytes=64)
+        xs = keep.tile([P, T], U8, name="xs", align_bytes=64)
+        w2w = keep.tile([P, 2 * N], U8, name="w2w", align_bytes=64)
+        w2s = keep.tile([P, N], U8, name="w2s", align_bytes=64)
+        warm_in = keep.tile([P, 8], F32, name="warm_in")
+        warm_out = keep.tile([P, 8], F32, name="warm_out")
+
+        nc.vector.memset(xs[:].bitcast(I32), 0)
+        nc.gpsimd.memset(w2s[:].bitcast(I32), 0)
+        nc.gpsimd.memset(warm_in[:], 0.0)
+        nc.scalar.activation(warm_out[:], warm_in[:], ACT.Sigmoid)
+
+        w1_rows = w1.rearrange("(p j) c -> p j c", j=PACK)
+        w1_raw = [keep.tile([P, PACK, H // 2], F32, name="w1_raw%d" % h, align_bytes=64) for h in range(2)]
+        nc.sync.dma_start(offs_t[:], offs)
+        nc.sync.dma_start(w1_raw[0][:], w1_rows[:, :, : H // 2])
+        for q in range(4):
+            nc.sync.dma_start(xs[32 * q : 32 * q + 4, :].bitcast(I32), x_scales[0, 4 * q : 4 * q + 4, :].bitcast(I32))
+        nc.sync.dma_start(w1_raw[1][:], w1_rows[:, :, H // 2 :])
+        nc.sync.dma_start(xw[:], x_words[0].rearrange("p c r -> p (c r)").bitcast(I32))
+        nc.sync.dma_start(w2w[:].bitcast(I32), w2_words[0].bitcast(I32))
+        nc.sync.dma_start(nb_t[:], nb)
+        for q in range(4):
+            nc.sync.dma_start(w2s[32 * q : 32 * q + 4, :].bitcast(I32), w2_scales[0, 4 * q : 4 * q + 4, :].bitcast(I32))
+        nc.sync.dma_start(slot_t[:], slot)
+        pg_rows = pg.rearrange("(p t) w -> p t w", t=PACK)
+        page = []
+        for t in range(PACK):
+            pt = keep.tile([P, U], F32, name="page%d" % t, align_bytes=64)
+            nc.sync.dma_start(pt[:], pg_rows[:, t, :])
+            page.append(pt)
+
+        xsg = keep.tile([P, S], U8, name="xsg", align_bytes=64)
+        nc.vector.tensor_copy(xsg[:], xs[:].indirect(offs_t[:]))
+
+        w1g = keep.tile([P, PACK, P, PACK], BF16, name="w1g", align_bytes=64)
+        for h in range(2):
+            (nc.scalar.copy if h == 0 else nc.vector.tensor_copy)(
+                w1g[:, :, h * 64 : (h + 1) * 64, :].rearrange("p t m j -> p m j t"),
+                w1_raw[h][:].rearrange("p j (m t) -> p m j t", t=PACK),
+            )
+        w1c = keep.tile([P, H], U32, name="w1c", align_bytes=64)
+        w1s = keep.tile([P, H], U8, name="w1s", align_bytes=64)
+        nc.vector.quantize_mx(
+            out=w1c[:].bitcast(FP8X4), scales=w1s[:], in_=w1g[:].rearrange("p t m j -> p (t m j)")
+        )
+
+        ybank = [[psum.tile([P, 2, HALF], F32, name="ybank%d%d" % (h, u)) for u in range(2)] for h in range(2)]
+        for h in range(2):
+            xg = keep.tile([P, HALF], U32, name="xg%d" % h, align_bytes=64)
+            nc.vector.tensor_copy(xg[:], xw[:].bitcast(U32).indirect(offs_t[:, h * 16 : (h + 1) * 16]))
+            for t in range(PACK):
+                cols = slice(t * P, (t + 1) * P)
+                nc.tensor.matmul_mx(
+                    out=ybank[h][t // 2][:, t % 2, :], lhsT=w1c[:, cols].bitcast(FP8X4), lhsT_scale=w1s[:, cols],
+                    rhs=xg[:].bitcast(FP8X4), rhs_scale=xsg[:, h * HALF : (h + 1) * HALF], start=True, stop=True,
+                )
+
+        ywin = [keep.tile([P, S], F32, name="ywin%d" % t, align_bytes=64) for t in range(PACK)]
+        yown = keep.tile([P, PACK, S], F32, name="yown", align_bytes=64)
+        for u in range(2):
+            for h in range(2):
+                for t in (2 * u, 2 * u + 1):
+                    nc.scalar.copy(ywin[t][:, h * HALF : (h + 1) * HALF], ybank[h][u][:, t % 2, :])
+            for t in (2 * u, 2 * u + 1):
+                nc.vector.tensor_copy(yown[:, t, :HALF], ywin[t][:, :HALF])
+
+        w2wd = keep.tile([P, 2 * N], U8, name="w2wd", align_bytes=64)
+        w2sd = keep.tile([P, N], U8, name="w2sd", align_bytes=64)
+        nc.vector.tensor_copy(
+            w2wd[:].rearrange("p (t m b) -> p m t b", t=PACK, b=2), w2w[:].rearrange("p (m t b) -> p m t b", t=PACK, b=2)
+        )
+        nc.vector.tensor_copy(
+            w2sd[:].rearrange("p (t m) -> p m t", t=PACK), w2s[:].rearrange("p (m t) -> p m t", t=PACK)
+        )
+
+        sig = keep.tile([P, PACK, S], F32, name="sig", align_bytes=64)
+        hs = keep.tile([P, PACK, S], F32, name="hs", align_bytes=64)
+        prod = [keep.tile([P, S], F32, name="prod%d" % t, align_bytes=64) for t in range(PACK)]
+        hbank = [[psum.tile([P, 2, HALF], F32, name="hbank%d%d" % (h, u)) for u in range(2)] for h in range(2)]
+
+        for c in range(4):
+            cols = slice(c * QUARTER, (c + 1) * QUARTER)
+            if c == 2:
+                for u in range(2):
+                    nc.scalar.copy(yown[:, 2 * u : 2 * u + 2, HALF:], ybank[1][u][:])
+            zneg = keep.tile([P, PACK, QUARTER], F32, name="zneg%d" % c, tag="zneg%d" % c if c < 2 else "zb%d" % (c - 2), align_bytes=64)
+            for t in range(PACK):
+                nc.vector.tensor_tensor(
+                    zneg[:, t, :], ywin[t][:].indirect(nb_t[:, c * 8 : (c + 1) * 8]), yown[:, t, cols], ALU.subtract
+                )
+            zb = keep.tile([P, QUARTER, PACK], BF16, name="zb%d" % c, tag="zb%d" % c, align_bytes=64)
+            nc.scalar.activation(
+                zb[:].rearrange("p (c i) t -> p c t i", i=4), zneg[:].rearrange("p t (c i) -> p c t i", i=4),
+                ACT.Copy, scale=-1.0,
+            )
+            zc = keep.tile([P, QUARTER], U32, name="zc%d" % c, align_bytes=64)
+            zs = keep.tile([P, QUARTER], U8, name="zs%d" % c, align_bytes=64)
+            nc.vector.quantize_mx(out=zc[:].bitcast(FP8X4), scales=zs[:], in_=zb[:].rearrange("p c t -> p (c t)"))
+            for t in range(PACK):
+                nc.tensor.matmul_mx(
+                    out=hbank[c // 2][t // 2][:, t % 2, (c % 2) * QUARTER : (c % 2 + 1) * QUARTER], lhsT=w2wd[:, 2 * t * P : 2 * (t + 1) * P].bitcast(FP4X4),
+                    lhsT_scale=w2sd[:, t * P : (t + 1) * P],
+                    rhs=zc[:].bitcast(FP8X4), rhs_scale=zs[:], start=True, stop=True,
+                )
+            if c == 1:
+                for u in range(2):
+                    nc.scalar.activation(sig[:, 2 * u : 2 * u + 2, :HALF], hbank[0][u][:], ACT.Sigmoid)
+        for u in range(2):
+            nc.scalar.activation(sig[:, 2 * u : 2 * u + 2, HALF:], hbank[1][u][:], ACT.Sigmoid)
+            for h in range(2):
+                nc.scalar.copy(hs[:, 2 * u : 2 * u + 2, h * HALF : (h + 1) * HALF], hbank[h][u][:])
+
+        def old_times_sig(h, t):
+            cols = slice(h * HALF, (h + 1) * HALF)
+            nc.vector.tensor_tensor(
+                prod[t][:, cols], page[t][:].indirect(slot_t[:, h * 16 : (h + 1) * 16]), sig[:, t, cols], ALU.mult
+            )
+
+        for t in range(PACK):
+            old_times_sig(0, t)
+
+        out_rows = out_0.rearrange("(p t) w -> p t w", t=PACK)
+        ob = keep.tile([P, U, PACK], BF16, name="ob", align_bytes=64)
+        old_times_sig(1, 0)
+        for t in range(PACK):
+            if t + 1 < PACK:
+                old_times_sig(1, t + 1)
+            nc.vector.tensor_tensor(page[t][:].indirect(slot_t[:]), hs[:, t, :], prod[t][:], ALU.add)
+            nc.sync.dma_start(out_rows[:, t, :], page[t][:])
+            if t < 2:
+                nc.scalar.copy(ob[:, :, t], page[t][:])
+            elif t == 2:
+                nc.scalar.copy(ob[:, : U // 2, 2:4], page[t][:, : U // 2].unsqueeze(2).to_broadcast([P, U // 2, 2]))
+                nc.scalar.copy(ob[:, U // 2 :, 2], page[t][:, U // 2 :])
+
+        oc = keep.tile([P, U], I32, name="oc", align_bytes=64)
+        osc = keep.tile([P, U], U8, name="osc", align_bytes=64)
+        words_out = out_1[0].rearrange("p c r -> p (c r)").bitcast(I32)
+        for c in range(4):
+            cols = slice(c * CHUNK, (c + 1) * CHUNK)
+            if c < 2:
+                nc.vector.tensor_copy(ob[:, cols, 3], page[3][:, cols])
+            else:
+                nc.scalar.copy(ob[:, cols, 3], page[3][:, cols])
+        for c in range(4):
+            cols = slice(c * CHUNK, (c + 1) * CHUNK)
+            nc.vector.quantize_mx(
+                out=oc[:, cols].bitcast(FP8X4), scales=osc[:, cols], in_=ob[:, cols, :].rearrange("p c t -> p (c t)")
+            )
+            if c % 2 == 1:
+                both = slice((c - 1) * CHUNK, (c + 1) * CHUNK)
+                nc.sync.dma_start(words_out[:, both], oc[:, both])
+        for q in range(4):
+            eng = nc.scalar if q % 2 == 0 else nc.sync
+            eng.dma_start(out_2[0, 4 * q : 4 * q + 4, :].bitcast(I32), osc[32 * q : 32 * q + 4, :].bitcast(I32))

@@ -47,12 +47,12 @@ def tile_picked_pagefly_none_po_kernel(
         nc.scalar.activation(warm_out[:], warm_in[:], ACT.Sigmoid)
 
         w1_rows = w1.rearrange("(p j) c -> p j c", j=PACK)
-        w1_raw = [keep.tile([P, PACK, H // 2], F32, name="w1_raw%d" % h, align_bytes=64) for h in range(2)]
+        w1_raw = keep.tile([P, PACK, H], F32, name="w1_raw", align_bytes=64)
         nc.sync.dma_start(offs_t[:], offs)
-        nc.sync.dma_start(w1_raw[0][:], w1_rows[:, :, : H // 2])
+        nc.sync.dma_start(w1_raw[:, :2, :], w1_rows[:, :2, :])
         for q in range(4):
             nc.sync.dma_start(xs[32 * q : 32 * q + 4, :].bitcast(I32), x_scales[0, 4 * q : 4 * q + 4, :].bitcast(I32))
-        nc.sync.dma_start(w1_raw[1][:], w1_rows[:, :, H // 2 :])
+        nc.sync.dma_start(w1_raw[:, 2:, :], w1_rows[:, 2:, :])
         nc.sync.dma_start(xw[:], x_words[0].rearrange("p c r -> p (c r)").bitcast(I32))
         nc.sync.dma_start(w2w[:].bitcast(I32), w2_words[0].bitcast(I32))
         nc.sync.dma_start(nb_t[:], nb)
@@ -70,10 +70,10 @@ def tile_picked_pagefly_none_po_kernel(
         nc.vector.tensor_copy(xsg[:], xs[:].indirect(offs_t[:]))
 
         w1g = keep.tile([P, PACK, P, PACK], BF16, name="w1g", align_bytes=64)
-        for h in range(2):
-            (nc.scalar.copy if h == 0 else nc.vector.tensor_copy)(
-                w1g[:, :, h * 64 : (h + 1) * 64, :].rearrange("p t m j -> p m j t"),
-                w1_raw[h][:].rearrange("p j (m t) -> p m j t", t=PACK),
+        for copy, lo, hi in ((nc.scalar.copy, 0, 48), (nc.vector.tensor_copy, 48, P)):
+            copy(
+                w1g[:, :, lo:hi, :].rearrange("p t m j -> p m j t"),
+                w1_raw[:, :, PACK * lo : PACK * hi].rearrange("p j (m t) -> p m j t", t=PACK),
             )
         w1c = keep.tile([P, H], U32, name="w1c", align_bytes=64)
         w1s = keep.tile([P, H], U8, name="w1s", align_bytes=64)
@@ -81,30 +81,34 @@ def tile_picked_pagefly_none_po_kernel(
             out=w1c[:].bitcast(FP8X4), scales=w1s[:], in_=w1g[:].rearrange("p t m j -> p (t m j)")
         )
 
-        ybank = [[psum.tile([P, 2, HALF], F32, name="ybank%d%d" % (h, u)) for u in range(2)] for h in range(2)]
+        pair_bank = [psum.tile([P, 2, HALF], F32, name="pair_bank%d" % h, tag="pair_bank%d" % h) for h in range(2)]
+        row_bank = [psum.tile([P, S], F32, name="row_bank%d" % t) for t in range(2)]
+
+        def y_psum(h, t):
+            return pair_bank[h][:, t, :] if t < 2 else row_bank[t - 2][:, h * HALF : (h + 1) * HALF]
+
         for h in range(2):
             xg = keep.tile([P, HALF], U32, name="xg%d" % h, align_bytes=64)
             nc.vector.tensor_copy(xg[:], xw[:].bitcast(U32).indirect(offs_t[:, h * 16 : (h + 1) * 16]))
             for t in range(PACK):
                 cols = slice(t * P, (t + 1) * P)
                 nc.tensor.matmul_mx(
-                    out=ybank[h][t // 2][:, t % 2, :], lhsT=w1c[:, cols].bitcast(FP8X4), lhsT_scale=w1s[:, cols],
+                    out=y_psum(h, t), lhsT=w1c[:, cols].bitcast(FP8X4), lhsT_scale=w1s[:, cols],
                     rhs=xg[:].bitcast(FP8X4), rhs_scale=xsg[:, h * HALF : (h + 1) * HALF], start=True, stop=True,
                 )
 
         ywin = [keep.tile([P, S], F32, name="ywin%d" % t, align_bytes=64) for t in range(PACK)]
-        yown = keep.tile([P, PACK, S], F32, name="yown", align_bytes=64)
-        for u in range(2):
-            for h in range(2):
-                for t in (2 * u, 2 * u + 1):
-                    nc.scalar.copy(ywin[t][:, h * HALF : (h + 1) * HALF], ybank[h][u][:, t % 2, :])
-            for t in (2 * u, 2 * u + 1):
-                nc.vector.tensor_copy(yown[:, t, :HALF], ywin[t][:, :HALF])
+        yown = [keep.tile([P, PACK, HALF], F32, name="yown%d" % h, align_bytes=64) for h in range(2)]
+        for h in range(2):
+            for t in range(2):
+                nc.scalar.copy(ywin[t][:, h * HALF : (h + 1) * HALF], y_psum(h, t))
+        for t in range(2, PACK):
+            nc.scalar.copy(ywin[t][:], row_bank[t - 2][:])
 
         w2wd = keep.tile([P, 2 * N], U8, name="w2wd", align_bytes=64)
         w2sd = keep.tile([P, N], U8, name="w2sd", align_bytes=64)
         nc.vector.tensor_copy(
-            w2wd[:].rearrange("p (t m b) -> p m t b", t=PACK, b=2), w2w[:].rearrange("p (m t b) -> p m t b", t=PACK, b=2)
+            w2wd[:].bitcast(U16).rearrange("p (t m) -> p m t", t=PACK), w2w[:].bitcast(U16).rearrange("p (m t) -> p m t", t=PACK)
         )
         nc.vector.tensor_copy(
             w2sd[:].rearrange("p (t m) -> p m t", t=PACK), w2s[:].rearrange("p (m t) -> p m t", t=PACK)
@@ -112,56 +116,69 @@ def tile_picked_pagefly_none_po_kernel(
 
         sig = keep.tile([P, PACK, S], F32, name="sig", align_bytes=64)
         hs = keep.tile([P, PACK, S], F32, name="hs", align_bytes=64)
-        prod = [keep.tile([P, S], F32, name="prod%d" % t, align_bytes=64) for t in range(PACK)]
-        hbank = [[psum.tile([P, 2, HALF], F32, name="hbank%d%d" % (h, u)) for u in range(2)] for h in range(2)]
+        groups = ((0, 1), (1, 2), (2, 4))
+        hbank = {}
 
-        for c in range(4):
-            cols = slice(c * QUARTER, (c + 1) * QUARTER)
-            if c == 2:
-                for u in range(2):
-                    nc.scalar.copy(yown[:, 2 * u : 2 * u + 2, HALF:], ybank[1][u][:])
-            zneg = keep.tile([P, PACK, QUARTER], F32, name="zneg%d" % c, tag="zneg%d" % c if c < 2 else "zb%d" % (c - 2), align_bytes=64)
-            for t in range(PACK):
-                nc.vector.tensor_tensor(
-                    zneg[:, t, :], ywin[t][:].indirect(nb_t[:, c * 8 : (c + 1) * 8]), yown[:, t, cols], ALU.subtract
-                )
-            zb = keep.tile([P, QUARTER, PACK], BF16, name="zb%d" % c, tag="zb%d" % c, align_bytes=64)
-            nc.scalar.activation(
-                zb[:].rearrange("p (c i) t -> p c t i", i=4), zneg[:].rearrange("p t (c i) -> p c t i", i=4),
-                ACT.Copy, scale=-1.0,
-            )
-            zc = keep.tile([P, QUARTER], U32, name="zc%d" % c, align_bytes=64)
-            zs = keep.tile([P, QUARTER], U8, name="zs%d" % c, align_bytes=64)
-            nc.vector.quantize_mx(out=zc[:].bitcast(FP8X4), scales=zs[:], in_=zb[:].rearrange("p c t -> p (c t)"))
-            for t in range(PACK):
-                nc.tensor.matmul_mx(
-                    out=hbank[c // 2][t // 2][:, t % 2, (c % 2) * QUARTER : (c % 2 + 1) * QUARTER], lhsT=w2wd[:, 2 * t * P : 2 * (t + 1) * P].bitcast(FP4X4),
-                    lhsT_scale=w2sd[:, t * P : (t + 1) * P],
-                    rhs=zc[:].bitcast(FP8X4), rhs_scale=zs[:], start=True, stop=True,
-                )
-            if c == 1:
-                for u in range(2):
-                    nc.scalar.activation(sig[:, 2 * u : 2 * u + 2, :HALF], hbank[0][u][:], ACT.Sigmoid)
-        for u in range(2):
-            nc.scalar.activation(sig[:, 2 * u : 2 * u + 2, HALF:], hbank[1][u][:], ACT.Sigmoid)
-            for h in range(2):
-                nc.scalar.copy(hs[:, 2 * u : 2 * u + 2, h * HALF : (h + 1) * HALF], hbank[h][u][:])
-
-        def old_times_sig(h, t):
+        for h in range(2):
             cols = slice(h * HALF, (h + 1) * HALF)
+            if h == 1:
+                nc.scalar.copy(yown[1][:, :2, :], pair_bank[1][:])
+                for t in range(2, PACK):
+                    nc.scalar.copy(yown[1][:, t, :], y_psum(1, t))
+            zb = keep.tile([P, HALF, PACK], BF16, name="zb%d" % h, tag="zb%d" % h, align_bytes=64)
+            for u in range(2):
+                tag = "zb0" if (h, u) == (1, 1) else "zneg%d%d" % (h, u)
+                zneg = keep.tile([P, 2, HALF], F32, name="zneg%d%d" % (h, u), tag=tag, align_bytes=64)
+                if h == 0:
+                    for t in (2 * u, 2 * u + 1):
+                        nc.vector.tensor_copy(yown[0][:, t, :], ywin[t][:, :HALF])
+                for t in (2 * u, 2 * u + 1):
+                    nc.vector.tensor_tensor(
+                        zneg[:, t % 2, :], ywin[t][:].indirect(nb_t[:, h * 16 : (h + 1) * 16]), yown[h][:, t, :], ALU.subtract
+                    )
+                nc.scalar.activation(
+                    zb[:, :, 2 * u : 2 * u + 2], zneg[:].rearrange("p t c -> p c t"), ACT.Copy, scale=-1.0
+                )
+            zc = keep.tile([P, HALF], U32, name="zc%d" % h, align_bytes=64)
+            zs = keep.tile([P, HALF], U8, name="zs%d" % h, align_bytes=64)
+            nc.vector.quantize_mx(out=zc[:].bitcast(FP8X4), scales=zs[:], in_=zb[:].rearrange("p c t -> p (c t)"))
+            for lo, hi in groups:
+                tag = "pair_bank%d" % h if lo == 0 else "hbank%d%d" % (h, lo)
+                bank = psum.tile([P, hi - lo, HALF], F32, name="hbank%d%d" % (h, lo), tag=tag)
+                hbank.setdefault((h, lo), bank)
+                for t in range(lo, hi):
+                    nc.tensor.matmul_mx(
+                        out=bank[:, t - lo, :], lhsT=w2wd[:, 2 * t * P : 2 * (t + 1) * P].bitcast(FP4X4),
+                        lhsT_scale=w2sd[:, t * P : (t + 1) * P],
+                        rhs=zc[:].bitcast(FP8X4), rhs_scale=zs[:], start=True, stop=True,
+                    )
+            if h == 0:
+                for lo, hi in groups:
+                    nc.scalar.activation(sig[:, lo:hi, cols], hbank[h, lo][:], ACT.Sigmoid)
+        for lo, hi in groups:
+            nc.scalar.activation(sig[:, lo:hi, HALF:], hbank[1, lo][:], ACT.Sigmoid)
+            for h in range(2):
+                nc.scalar.copy(hs[:, lo:hi, h * HALF : (h + 1) * HALF], hbank[h, lo][:])
+
+        prod = [
+            keep.tile([P, S], F32, name="prod%d" % t, tag="zb1" if t == 2 else "prod%d" % t, align_bytes=64)
+            for t in range(PACK)
+        ]
+
+        def old_times_sig(t, lo, hi):
             nc.vector.tensor_tensor(
-                prod[t][:, cols], page[t][:].indirect(slot_t[:, h * 16 : (h + 1) * 16]), sig[:, t, cols], ALU.mult
+                prod[t][:, lo:hi], page[t][:].indirect(slot_t[:, lo // 16 : hi // 16]), sig[:, t, lo:hi], ALU.mult
             )
 
         for t in range(PACK):
-            old_times_sig(0, t)
+            old_times_sig(t, 0, HALF)
 
         out_rows = out_0.rearrange("(p t) w -> p t w", t=PACK)
         ob = keep.tile([P, U, PACK], BF16, name="ob", align_bytes=64)
-        old_times_sig(1, 0)
+        old_times_sig(0, HALF, S)
         for t in range(PACK):
             if t + 1 < PACK:
-                old_times_sig(1, t + 1)
+                old_times_sig(t + 1, HALF, S)
             nc.vector.tensor_tensor(page[t][:].indirect(slot_t[:]), hs[:, t, :], prod[t][:], ALU.add)
             nc.sync.dma_start(out_rows[:, t, :], page[t][:])
             if t < 2:
@@ -184,9 +201,9 @@ def tile_picked_pagefly_none_po_kernel(
             nc.vector.quantize_mx(
                 out=oc[:, cols].bitcast(FP8X4), scales=osc[:, cols], in_=ob[:, cols, :].rearrange("p c t -> p (c t)")
             )
-            if c % 2 == 1:
-                both = slice((c - 1) * CHUNK, (c + 1) * CHUNK)
-                nc.sync.dma_start(words_out[:, both], oc[:, both])
+            if c > 0:
+                done = slice(0 if c == 1 else c * CHUNK, (c + 1) * CHUNK)
+                nc.sync.dma_start(words_out[:, done], oc[:, done])
         for q in range(4):
             eng = nc.scalar if q % 2 == 0 else nc.sync
             eng.dma_start(out_2[0, 4 * q : 4 * q + 4, :].bitcast(I32), osc[32 * q : 32 * q + 4, :].bitcast(I32))

@@ -38,9 +38,9 @@ def tile_picked_pagefly_none_po_kernel(
         xs = keep.tile([P, T], U8, name="xs", align_bytes=64)
         w2w = keep.tile([P, 2 * N], U8, name="w2w", align_bytes=64)
         w2s = keep.tile([P, N], U8, name="w2s", align_bytes=64)
+
         warm_in = keep.tile([P, 8], F32, name="warm_in")
         warm_out = keep.tile([P, 8], F32, name="warm_out")
-
         nc.vector.memset(xs[:].bitcast(I32), 0)
         nc.gpsimd.memset(w2s[:].bitcast(I32), 0)
         nc.gpsimd.memset(warm_in[:], 0.0)
@@ -70,11 +70,15 @@ def tile_picked_pagefly_none_po_kernel(
         nc.vector.tensor_copy(xsg[:], xs[:].indirect(offs_t[:]))
 
         w1g = keep.tile([P, PACK, P, PACK], BF16, name="w1g", align_bytes=64)
-        for copy, lo, hi in ((nc.scalar.copy, 0, 48), (nc.vector.tensor_copy, 48, P)):
-            copy(
-                w1g[:, :, lo:hi, :].rearrange("p t m j -> p m j t"),
-                w1_raw[:, :, PACK * lo : PACK * hi].rearrange("p j (m t) -> p m j t", t=PACK),
-            )
+        split = 48
+        nc.scalar.copy(
+            w1g[:, :, :split, :].rearrange("p t m j -> p m j t"),
+            w1_raw[:, :, : PACK * split].rearrange("p j (m t) -> p m j t", t=PACK),
+        )
+        nc.vector.tensor_copy(
+            w1g[:, :, split:, :].rearrange("p t m j -> p m j t"),
+            w1_raw[:, :, PACK * split :].rearrange("p j (m t) -> p m j t", t=PACK),
+        )
         w1c = keep.tile([P, H], U32, name="w1c", align_bytes=64)
         w1s = keep.tile([P, H], U8, name="w1s", align_bytes=64)
         nc.vector.quantize_mx(
@@ -104,6 +108,8 @@ def tile_picked_pagefly_none_po_kernel(
                 nc.scalar.copy(ywin[t][:, h * HALF : (h + 1) * HALF], y_psum(h, t))
         for t in range(2, PACK):
             nc.scalar.copy(ywin[t][:], row_bank[t - 2][:])
+            nc.scalar.copy(yown[0][:, t, :], y_psum(0, t))
+        nc.scalar.copy(yown[1][:, :2, :], pair_bank[1][:])
 
         w2wd = keep.tile([P, 2 * N], U8, name="w2wd", align_bytes=64)
         w2sd = keep.tile([P, N], U8, name="w2sd", align_bytes=64)
@@ -122,15 +128,14 @@ def tile_picked_pagefly_none_po_kernel(
         for h in range(2):
             cols = slice(h * HALF, (h + 1) * HALF)
             if h == 1:
-                nc.scalar.copy(yown[1][:, :2, :], pair_bank[1][:])
                 for t in range(2, PACK):
                     nc.scalar.copy(yown[1][:, t, :], y_psum(1, t))
             zb = keep.tile([P, HALF, PACK], BF16, name="zb%d" % h, tag="zb%d" % h, align_bytes=64)
             for u in range(2):
                 tag = "zb0" if (h, u) == (1, 1) else "zneg%d%d" % (h, u)
                 zneg = keep.tile([P, 2, HALF], F32, name="zneg%d%d" % (h, u), tag=tag, align_bytes=64)
-                if h == 0:
-                    for t in (2 * u, 2 * u + 1):
+                if (h, u) == (0, 0):
+                    for t in range(2):
                         nc.vector.tensor_copy(yown[0][:, t, :], ywin[t][:, :HALF])
                 for t in (2 * u, 2 * u + 1):
                     nc.vector.tensor_tensor(

@@ -48,8 +48,8 @@ def tile_picked_pagefly_none_po_kernel(
 
         w1_rows = w1.rearrange("(p j) c -> p j c", j=PACK)
         w1_raw = keep.tile([P, PACK, H], F32, name="w1_raw", align_bytes=64)
-        nc.sync.dma_start(offs_t[:], offs)
         nc.sync.dma_start(w1_raw[:, :2, :], w1_rows[:, :2, :])
+        nc.sync.dma_start(offs_t[:], offs)
         for q in range(4):
             nc.sync.dma_start(xs[32 * q : 32 * q + 4, :].bitcast(I32), x_scales[0, 4 * q : 4 * q + 4, :].bitcast(I32))
         nc.sync.dma_start(w1_raw[:, 2:, :], w1_rows[:, 2:, :])
@@ -91,15 +91,15 @@ def tile_picked_pagefly_none_po_kernel(
         def y_psum(h, t):
             return pair_bank[h][:, t, :] if t < 2 else row_bank[t - 2][:, h * HALF : (h + 1) * HALF]
 
+        xg = [keep.tile([P, HALF], U32, name="xg%d" % h, align_bytes=64) for h in range(2)]
         for h in range(2):
-            xg = keep.tile([P, HALF], U32, name="xg%d" % h, align_bytes=64)
-            nc.vector.tensor_copy(xg[:], xw[:].bitcast(U32).indirect(offs_t[:, h * 16 : (h + 1) * 16]))
-            for t in range(PACK):
-                cols = slice(t * P, (t + 1) * P)
-                nc.tensor.matmul_mx(
-                    out=y_psum(h, t), lhsT=w1c[:, cols].bitcast(FP8X4), lhsT_scale=w1s[:, cols],
-                    rhs=xg[:].bitcast(FP8X4), rhs_scale=xsg[:, h * HALF : (h + 1) * HALF], start=True, stop=True,
-                )
+            nc.vector.tensor_copy(xg[h][:], xw[:].bitcast(U32).indirect(offs_t[:, h * 16 : (h + 1) * 16]))
+        for h, t in [(h, t) for h in range(2) for t in range(2)] + [(h, t) for t in range(2, PACK) for h in range(2)]:
+            cols = slice(t * P, (t + 1) * P)
+            nc.tensor.matmul_mx(
+                out=y_psum(h, t), lhsT=w1c[:, cols].bitcast(FP8X4), lhsT_scale=w1s[:, cols],
+                rhs=xg[h][:].bitcast(FP8X4), rhs_scale=xsg[:, h * HALF : (h + 1) * HALF], start=True, stop=True,
+            )
 
         ywin = [keep.tile([P, S], F32, name="ywin%d" % t, align_bytes=64) for t in range(PACK)]
         yown = [keep.tile([P, PACK, HALF], F32, name="yown%d" % h, align_bytes=64) for h in range(2)]
@@ -195,20 +195,15 @@ def tile_picked_pagefly_none_po_kernel(
         oc = keep.tile([P, U], I32, name="oc", align_bytes=64)
         osc = keep.tile([P, U], U8, name="osc", align_bytes=64)
         words_out = out_1[0].rearrange("p c r -> p (c r)").bitcast(I32)
-        for c in range(4):
+        nc.vector.tensor_copy(ob[:, : U // 2, 3], page[3][:, : U // 2])
+        for c in (2, 3):
             cols = slice(c * CHUNK, (c + 1) * CHUNK)
-            if c < 2:
-                nc.vector.tensor_copy(ob[:, cols, 3], page[3][:, cols])
-            else:
-                nc.scalar.copy(ob[:, cols, 3], page[3][:, cols])
-        for c in range(4):
-            cols = slice(c * CHUNK, (c + 1) * CHUNK)
+            nc.scalar.copy(ob[:, cols, 3], page[3][:, cols])
+        for lo, hi in ((2 * CHUNK, 3 * CHUNK), (0, 2 * CHUNK), (3 * CHUNK, U)):
             nc.vector.quantize_mx(
-                out=oc[:, cols].bitcast(FP8X4), scales=osc[:, cols], in_=ob[:, cols, :].rearrange("p c t -> p (c t)")
+                out=oc[:, lo:hi].bitcast(FP8X4), scales=osc[:, lo:hi], in_=ob[:, lo:hi, :].rearrange("p c t -> p (c t)")
             )
-            if c > 0:
-                done = slice(0 if c == 1 else c * CHUNK, (c + 1) * CHUNK)
-                nc.sync.dma_start(words_out[:, done], oc[:, done])
+            nc.sync.dma_start(words_out[:, lo:hi], oc[:, lo:hi])
         for q in range(4):
             eng = nc.scalar if q % 2 == 0 else nc.sync
             eng.dma_start(out_2[0, 4 * q : 4 * q + 4, :].bitcast(I32), osc[32 * q : 32 * q + 4, :].bitcast(I32))

from contextlib import ExitStack

import concourse.mybir as mybir

K, T, S, N, U, H = 512, 2048, 512, 512, 1024, 512
FLOPS = 2 * K * H * S + 2 * H * N * S

F32 = mybir.dt.float32
BF16 = mybir.dt.bfloat16
I32 = mybir.dt.int32
U32 = mybir.dt.uint32
U16 = mybir.dt.uint16
U8 = mybir.dt.uint8
FP8X4 = mybir.dt.float8_e4m3fn_x4
FP4X4 = mybir.dt.float4_e2m1fn_x4
ALU = mybir.AluOpType
ACT = mybir.ActivationFunctionType

P = 128
PACK = 4
HALF = S // 2
QUARTER = S // 4
CHUNK = U // 4


def tile_picked_pagefly_none_po_kernel(
    tc, x_words, x_scales, w1, w2_words, w2_scales, pg, offs, nb, slot, out_0, out_1, out_2
):
    nc = tc.nc
    with ExitStack() as ctx:
        keep = ctx.enter_context(tc.tile_pool(name="keep", bufs=1))
        psum = ctx.enter_context(tc.psum_pool(name="psum", bufs=1))

        offs_t = keep.tile([P, S // 16], U16, name="offs_t")
        nb_t = keep.tile([P, S // 16], U16, name="nb_t")
        slot_t = keep.tile([P, S // 16], U16, name="slot_t")
        xw = keep.tile([P, T], I32, name="xw", align_bytes=64)
        xs = keep.tile([P, T], U8, name="xs", align_bytes=64)
        w2w = keep.tile([P, 2 * N], U8, name="w2w", align_bytes=64)
        w2s = keep.tile([P, N], U8, name="w2s", align_bytes=64)

        warm_in = keep.tile([P, 8], F32, name="warm_in")
        warm_out = keep.tile([P, 8], F32, name="warm_out")
        nc.vector.memset(xs[:].bitcast(I32), 0)
        nc.gpsimd.memset(w2s[:].bitcast(I32), 0)
        nc.gpsimd.memset(warm_in[:], 0.0)
        nc.scalar.activation(warm_out[:], warm_in[:], ACT.Sigmoid)

        w1_rows = w1.rearrange("(p j) c -> p j c", j=PACK)
        w1_raw = keep.tile([P, PACK, H], F32, name="w1_raw", align_bytes=64)
        nc.sync.dma_start(w1_raw[:, :2, :], w1_rows[:, :2, :])
        nc.sync.dma_start(offs_t[:], offs)
        for q in range(4):
            nc.sync.dma_start(xs[32 * q : 32 * q + 4, :].bitcast(I32), x_scales[0, 4 * q : 4 * q + 4, :].bitcast(I32))
        nc.sync.dma_start(w1_raw[:, 2:, :], w1_rows[:, 2:, :])
        nc.sync.dma_start(xw[:], x_words[0].rearrange("p c r -> p (c r)").bitcast(I32))
        nc.sync.dma_start(w2w[:].bitcast(I32), w2_words[0].bitcast(I32))
        nc.sync.dma_start(nb_t[:], nb)
        for q in range(4):
            nc.sync.dma_start(w2s[32 * q : 32 * q + 4, :].bitcast(I32), w2_scales[0, 4 * q : 4 * q + 4, :].bitcast(I32))
        nc.sync.dma_start(slot_t[:], slot)
        pg_rows = pg.rearrange("(p t) w -> p t w", t=PACK)
        page = []
        for t in range(PACK):
            pt = keep.tile([P, U], F32, name="page%d" % t, align_bytes=64)
            nc.sync.dma_start(pt[:], pg_rows[:, t, :])
            page.append(pt)

        xsg = keep.tile([P, S], U8, name="xsg", align_bytes=64)
        nc.vector.tensor_copy(xsg[:], xs[:].indirect(offs_t[:]))

        w1g = keep.tile([P, PACK, P, PACK], BF16, name="w1g", align_bytes=64)
        split = 48
        nc.scalar.copy(
            w1g[:, :, :split, :].rearrange("p t m j -> p m j t"),
            w1_raw[:, :, : PACK * split].rearrange("p j (m t) -> p m j t", t=PACK),
        )
        nc.vector.tensor_copy(
            w1g[:, :, split:, :].rearrange("p t m j -> p m j t"),
            w1_raw[:, :, PACK * split :].rearrange("p j (m t) -> p m j t", t=PACK),
        )
        w1c = keep.tile([P, H], U32, name="w1c", align_bytes=64)
        w1s = keep.tile([P, H], U8, name="w1s", align_bytes=64)
        nc.vector.quantize_mx(
            out=w1c[:].bitcast(FP8X4), scales=w1s[:], in_=w1g[:].rearrange("p t m j -> p (t m j)")
        )

        pair_bank = [psum.tile([P, 2, HALF], F32, name="pair_bank%d" % h, tag="pair_bank%d" % h) for h in range(2)]
        row_bank = [psum.tile([P, S], F32, name="row_bank%d" % t) for t in range(2)]

        def y_psum(h, t):
            return pair_bank[h][:, t, :] if t < 2 else row_bank[t - 2][:, h * HALF : (h + 1) * HALF]

        xg = [keep.tile([P, HALF], U32, name="xg%d" % h, align_bytes=64) for h in range(2)]
        for h in range(2):
            nc.vector.tensor_copy(xg[h][:], xw[:].bitcast(U32).indirect(offs_t[:, h * 16 : (h + 1) * 16]))
        for h, t in [(h, t) for h in range(2) for t in range(2)] + [(h, t) for t in range(2, PACK) for h in range(2)]:
            cols = slice(t * P, (t + 1) * P)
            nc.tensor.matmul_mx(
                out=y_psum(h, t), lhsT=w1c[:, cols].bitcast(FP8X4), lhsT_scale=w1s[:, cols],
                rhs=xg[h][:].bitcast(FP8X4), rhs_scale=xsg[:, h * HALF : (h + 1) * HALF], start=True, stop=True,
            )

        ywin = [keep.tile([P, S], F32, name="ywin%d" % t, align_bytes=64) for t in range(PACK)]
        yown = [keep.tile([P, PACK, HALF], F32, name="yown%d" % h, align_bytes=64) for h in range(2)]
        for h in range(2):
            for t in range(2):
                nc.scalar.copy(ywin[t][:, h * HALF : (h + 1) * HALF], y_psum(h, t))
        for t in range(2, PACK):
            nc.scalar.copy(ywin[t][:], row_bank[t - 2][:])
            nc.scalar.copy(yown[0][:, t, :], y_psum(0, t))
        nc.scalar.copy(yown[1][:, :2, :], pair_bank[1][:])

        w2wd = keep.tile([P, 2 * N], U8, name="w2wd", align_bytes=64)
        w2sd = keep.tile([P, N], U8, name="w2sd", align_bytes=64)
        nc.vector.tensor_copy(
            w2wd[:].bitcast(U16).rearrange("p (t m) -> p m t", t=PACK), w2w[:].bitcast(U16).rearrange("p (m t) -> p m t", t=PACK)
        )
        nc.vector.tensor_copy(
            w2sd[:].rearrange("p (t m) -> p m t", t=PACK), w2s[:].rearrange("p (m t) -> p m t", t=PACK)
        )

        sig = keep.tile([P, PACK, S], F32, name="sig", align_bytes=64)
        hs = keep.tile([P, PACK, S], F32, name="hs", align_bytes=64)
        groups = ((0, 1), (1, 2), (2, 4))
        hbank = {}

        for h in range(2):
            cols = slice(h * HALF, (h + 1) * HALF)
            if h == 1:
                for t in range(2, PACK):
                    nc.scalar.copy(yown[1][:, t, :], y_psum(1, t))
            zb = keep.tile([P, HALF, PACK], BF16, name="zb%d" % h, tag="zb%d" % h, align_bytes=64)
            for u in range(2):
                tag = "zb0" if (h, u) == (1, 1) else "zneg%d%d" % (h, u)
                zneg = keep.tile([P, 2, HALF], F32, name="zneg%d%d" % (h, u), tag=tag, align_bytes=64)
                if (h, u) == (0, 0):
                    for t in range(2):
                        nc.vector.tensor_copy(yown[0][:, t, :], ywin[t][:, :HALF])
                for t in (2 * u, 2 * u + 1):
                    nc.vector.tensor_tensor(
                        zneg[:, t % 2, :], ywin[t][:].indirect(nb_t[:, h * 16 : (h + 1) * 16]), yown[h][:, t, :], ALU.subtract
                    )
                nc.scalar.activation(
                    zb[:, :, 2 * u : 2 * u + 2], zneg[:].rearrange("p t c -> p c t"), ACT.Copy, scale=-1.0
                )
            zc = keep.tile([P, HALF], U32, name="zc%d" % h, align_bytes=64)
            zs = keep.tile([P, HALF], U8, name="zs%d" % h, align_bytes=64)
            nc.vector.quantize_mx(out=zc[:].bitcast(FP8X4), scales=zs[:], in_=zb[:].rearrange("p c t -> p (c t)"))
            for lo, hi in groups:
                tag = "pair_bank%d" % h if lo == 0 else "hbank%d%d" % (h, lo)
                bank = psum.tile([P, hi - lo, HALF], F32, name="hbank%d%d" % (h, lo), tag=tag)
                hbank.setdefault((h, lo), bank)
                for t in range(lo, hi):
                    nc.tensor.matmul_mx(
                        out=bank[:, t - lo, :], lhsT=w2wd[:, 2 * t * P : 2 * (t + 1) * P].bitcast(FP4X4),
                        lhsT_scale=w2sd[:, t * P : (t + 1) * P],
                        rhs=zc[:].bitcast(FP8X4), rhs_scale=zs[:], start=True, stop=True,
                    )
            if h == 0:
                for lo, hi in groups:
                    nc.scalar.activation(sig[:, lo:hi, cols], hbank[h, lo][:], ACT.Sigmoid)
        for lo, hi in groups:
            nc.scalar.activation(sig[:, lo:hi, HALF:], hbank[1, lo][:], ACT.Sigmoid)
            for h in range(2):
                nc.scalar.copy(hs[:, lo:hi, h * HALF : (h + 1) * HALF], hbank[h, lo][:])

        prod = [
            keep.tile([P, S], F32, name="prod%d" % t, tag="zb1" if t == 2 else "prod%d" % t, align_bytes=64)
            for t in range(PACK)
        ]

        def old_times_sig(t, lo, hi):
            nc.vector.tensor_tensor(
                prod[t][:, lo:hi], page[t][:].indirect(slot_t[:, lo // 16 : hi // 16]), sig[:, t, lo:hi], ALU.mult
            )

        for t in range(PACK):
            old_times_sig(t, 0, HALF)

        out_rows = out_0.rearrange("(p t) w -> p t w", t=PACK)
        ob = keep.tile([P, U, PACK], BF16, name="ob", align_bytes=64)
        old_times_sig(0, HALF, S)
        for t in range(PACK):
            if t + 1 < PACK:
                old_times_sig(t + 1, HALF, S)
            nc.vector.tensor_tensor(page[t][:].indirect(slot_t[:]), hs[:, t, :], prod[t][:], ALU.add)
            nc.sync.dma_start(out_rows[:, t, :], page[t][:])
            if t < 2:
                nc.scalar.copy(ob[:, :, t], page[t][:])
            elif t == 2:
                nc.scalar.copy(ob[:, : U // 2, 2:4], page[t][:, : U // 2].unsqueeze(2).to_broadcast([P, U // 2, 2]))
                nc.scalar.copy(ob[:, U // 2 :, 2], page[t][:, U // 2 :])

        oc = keep.tile([P, U], I32, name="oc", align_bytes=64)
        osc = keep.tile([P, U], U8, name="osc", align_bytes=64)
        words_out = out_1[0].rearrange("p c r -> p (c r)").bitcast(I32)
        nc.vector.tensor_copy(ob[:, : U // 2, 3], page[3][:, : U // 2])
        for c in (2, 3):
            cols = slice(c * CHUNK, (c + 1) * CHUNK)
            nc.scalar.copy(ob[:, cols, 3], page[3][:, cols])
        for lo, hi in ((2 * CHUNK, 3 * CHUNK), (0, 2 * CHUNK), (3 * CHUNK, U)):
            nc.vector.quantize_mx(
                out=oc[:, lo:hi].bitcast(FP8X4), scales=osc[:, lo:hi], in_=ob[:, lo:hi, :].rearrange("p c t -> p (c t)")
            )
            nc.sync.dma_start(words_out[:, lo:hi], oc[:, lo:hi])
        for q in range(4):
            eng = nc.scalar if q % 2 == 0 else nc.sync
            eng.dma_start(out_2[0, 4 * q : 4 * q + 4, :].bitcast(I32), osc[32 * q : 32 * q + 4, :].bitcast(I32))
